import numpy as np
import ml_dtypes


def mxq(x, axis, fmt="e4m3"):
    dtype, down = {"e4m3": (ml_dtypes.float8_e4m3fn, 7), "e5m2": (ml_dtypes.float8_e5m2, 14)}[fmt]
    v = np.moveaxis(np.asarray(x, np.float32).astype(ml_dtypes.bfloat16).astype(np.float64), axis, -1)
    blocks = v.reshape(v.shape[:-1] + (-1, 32))
    amax = np.abs(blocks).max(-1, keepdims=True)
    byte = np.maximum(np.where(amax > 0, np.frexp(amax)[1] - 1 + 127, 0) - down, 1)
    scale = np.exp2(byte - 127.0)
    codes = (blocks / scale).astype(np.float32).astype(dtype).astype(np.float64)
    return np.moveaxis((codes * scale).reshape(v.shape), -1, axis)


WIDE = False


def mx_kscale(k):
    if not WIDE:
        return np.ones(k)
    levels = np.array([10, -10, 5, -5, 0])
    if k % 512:
        return np.exp2(np.random.permutation(np.resize(levels, k // 32))).repeat(32)
    a = np.empty((k // 512, 16))
    for p in range(k // 512):
        a[p, :8] = np.random.permutation(np.resize(levels, 8))
        for g in range(8):
            far = levels[np.abs(levels - a[p, g]) >= 10]
            a[p, g + 8] = far[np.random.randint(len(far))]
    return np.exp2(a.ravel()).repeat(32)


def f64(x):
    return np.asarray(x).astype(np.float64)


def striped(idx):
    return np.tile(idx.reshape(-1, 16).T, (8, 1)).astype(np.uint16)


def unstriped(offs):
    return offs[:16].T.reshape(-1).astype(np.int64)


def pack_weight(w):
    k, n = w.shape
    w = f64(np.asarray(w, np.float32).astype(ml_dtypes.bfloat16)).reshape(k // 32, 32, n)
    amax = np.abs(w).max(1)
    byte = np.clip(np.where(amax > 0, np.frexp(amax)[1] - 1 + 127 - 7, 1), 1, 254)
    scaled = (w * np.exp2(127.0 - byte)[:, None, :]).reshape(k, n).astype(np.float32)
    words = np.ascontiguousarray(scaled.reshape(k // 512, 128, 4, n).transpose(0, 1, 3, 2)).astype(ml_dtypes.float8_e4m3fn).view(np.uint8)
    return words, np.ascontiguousarray(byte.astype(np.uint8).reshape(k // 512, 16, n))


def unpack_weight(words, scales):
    g, p, n, _ = words.shape
    vals = np.ascontiguousarray(words).view(ml_dtypes.float8_e4m3fn).astype(np.float64) * np.repeat(np.exp2(scales.astype(np.float64) - 127.0), 8, axis=1)[..., None]
    return vals.transpose(0, 1, 3, 2).reshape(g * 512, n)


E2M1 = np.array([0.0, 0.5, 1.0, 1.5, 2.0, 3.0, 4.0, 6.0, -0.0, -0.5, -1.0, -1.5, -2.0, -3.0, -4.0, -6.0])


def pack_fp4(w):
    k, n = w.shape
    w = f64(np.asarray(w, np.float32).astype(ml_dtypes.bfloat16)).reshape(k // 32, 32, n)
    amax = np.abs(w).max(1)
    mant, ex = np.frexp(amax / 6.0)
    byte = np.clip(np.where(amax > 0, np.where(mant > 0.5, ex, ex - 1) + 127, 1), 1, 254)
    scaled = (w * np.exp2(127.0 - byte)[:, None, :]).reshape(k, n).astype(np.float32)
    c = np.ascontiguousarray(scaled.reshape(k // 512, 128, 4, n).transpose(0, 1, 3, 2)).astype(ml_dtypes.float4_e2m1fn).view(np.uint8) & 0xF
    words = (c[..., 0::2] | (c[..., 1::2] << 4)).reshape(k // 512, 128, 2 * n)
    return np.ascontiguousarray(words), np.ascontiguousarray(byte.astype(np.uint8).reshape(k // 512, 16, n))


def unpack_fp4(words, scales):
    g, _, n = scales.shape
    words = np.ascontiguousarray(words).reshape(g, 128, n, 2)
    nib = np.empty((g, 128, n, 4), np.uint8)
    nib[..., 0::2] = words & 0xF
    nib[..., 1::2] = words >> 4
    vals = E2M1[nib] * np.repeat(np.exp2(scales.astype(np.float64) - 127.0), 8, axis=1)[..., None]
    return vals.transpose(0, 1, 3, 2).reshape(g * 512, n)


def planes(y):
    n, m = y.shape
    v = y.astype(np.float32).astype(ml_dtypes.bfloat16).astype(np.float64).reshape(n // 32, 32, m)
    top = np.abs(v).max(1)
    byte = np.clip(np.where(top > 0, np.frexp(top)[1] - 1 + 127 - 7, 1), 1, 254)
    codes = (v * np.exp2(127.0 - byte)[:, None, :]).reshape(n, m).astype(np.float32).astype(ml_dtypes.float8_e4m3fn).view(np.uint8)
    words = codes.reshape(n // 512, 128, 4, m).transpose(0, 1, 3, 2)
    return np.ascontiguousarray(words), np.ascontiguousarray(byte.astype(np.uint8).reshape(n // 512, 16, m))


K, T, S, N, H, U = 1024, 1024, 512, 512, 512, 1024


def setup_inputs():
    n = np.random.standard_normal
    s = mx_kscale(K)[:, None]
    u = mx_kscale(H)
    packed_xT = pack_weight(n((K, T)) * s)
    packed_w1 = pack_fp4(n((K, N)) / np.sqrt(K) / s)
    packed_w2 = pack_fp4(n((K, N)) / np.sqrt(K) / s)
    packed_w3 = pack_fp4(n((H, N)) / np.sqrt(H) / u[:, None])
    return {
        "x_words": packed_xT[0],
        "x_scales": packed_xT[1],
        "w1_words": packed_w1[0],
        "w1_scales": packed_w1[1],
        "w2_words": packed_w2[0],
        "w2_scales": packed_w2[1],
        "ref": (n((H, U))).astype(np.float32),
        "unit": (np.random.uniform(0.6, 1.4, (H, 1)) * u[:, None]).astype(np.float32),
        "w3_words": packed_w3[0],
        "w3_scales": packed_w3[1],
        "offs": striped(np.random.permutation(T)[:S]),
        "pa": striped(np.random.permutation(np.concatenate([np.arange(S), np.random.randint(0, S, U - S)]))),
        "pb": striped(np.random.permutation(np.concatenate([np.arange(S), np.random.randint(0, S, U - S)]))),
    }


def reference(x_words, x_scales, w1_words, w1_scales, w2_words, w2_scales, ref, unit, w3_words, w3_scales, offs, pa, pb):
    xq = unpack_weight(x_words, x_scales)[:, unstriped(offs)]
    y = unpack_fp4(w1_words, w1_scales).T @ xq
    ya = y[:, unstriped(pa)]
    yb_ = y[:, unstriped(pb)]
    z1 = unpack_fp4(w2_words, w2_scales).T @ xq
    za = z1[:, unstriped(pa)]
    zb_ = z1[:, unstriped(pb)]
    dot = ya * yb_ + za * zb_
    hid = f64(unit) * (dot - f64(ref))
    out_0 = unpack_fp4(w3_words, w3_scales).T @ mxq(hid, 0, "e4m3")
    return (out_0,) + planes(out_0)

@@ -1,0 +1,219 @@
+from contextlib import ExitStack
+
+import concourse.mybir as mybir
+from concourse.masks import make_identity
+
+K, T, S, H, N, U = 1024, 1024, 512, 512, 512, 1024
+FLOPS = 2 * K * H * S * 2 + 2 * H * N * U
+
+F32 = mybir.dt.float32
+BF16 = mybir.dt.bfloat16
+I32 = mybir.dt.int32
+U32 = mybir.dt.uint32
+U16 = mybir.dt.uint16
+U8 = mybir.dt.uint8
+FP8X4 = mybir.dt.float8_e4m3fn_x4
+FP4X4 = mybir.dt.float4_e2m1fn_x4
+MULT = mybir.AluOpType.mult
+COPY = mybir.ActivationFunctionType.Copy
+
+P = 128
+PASSES = K // 512
+CHUNKS = (384, 256, 256, 128)
+
+
+def tile_picked_ycrossp_dot_po_kernel(
+    tc, x_words, x_scales, w1_words, w1_scales, w2_words, w2_scales, ref, unit,
+    w3_words, w3_scales, offs, pa, pb, out_0, out_1, out_2,
+):
+    nc = tc.nc
+    with ExitStack() as ctx:
+        keep = ctx.enter_context(tc.tile_pool(name="keep", bufs=1))
+        psum = ctx.enter_context(tc.psum_pool(name="psum", bufs=1))
+
+        def sb(name, shape, dtype):
+            return keep.tile(shape, dtype, name=name, align_bytes=64)
+
+        def bank(b):
+            return psum.tile([P, 512], F32, name="bank%d" % b, tag="bank%d" % b)
+
+        def load_scales(queue, plane, scales):
+            for q in range(4):
+                queue.dma_start(
+                    out=plane[32 * q : 32 * q + 4, :, :].bitcast(I32),
+                    in_=scales[:, 4 * q : 4 * q + 4, :].rearrange("g q c -> q g c").bitcast(I32),
+                )
+
+        offs_t = sb("offs_t", [P, S // 16], U16)
+        pa_t = sb("pa_t", [P, U // 16], U16)
+        pb_t = sb("pb_t", [P, U // 16], U16)
+        xw = [sb("xw%d" % g, [P, T], I32) for g in range(PASSES)]
+        xs = sb("xs", [P, PASSES, T], U8)
+        ww = [sb("ww%d" % k, [P, PASSES, 2 * H], U8) for k in range(2)]
+        ws = [sb("ws%d" % k, [P, PASSES, H], U8) for k in range(2)]
+        w3w = sb("w3w", [P, 2 * N], U8)
+        w3s = sb("w3s", [P, 1, N], U8)
+        unit_t = sb("unit_t", [P, 4], F32)
+        ref_t = [sb("ref%d" % t, [P, U], F32) for t in range(4)]
+        ident = sb("ident", [P, P], F32)
+
+        nc.vector.memset(xs[:].bitcast(I32), 0)
+        nc.gpsimd.memset(ws[0][:].bitcast(I32), 0)
+        nc.gpsimd.memset(ws[1][:].bitcast(I32), 0)
+        nc.gpsimd.memset(w3s[:].bitcast(I32), 0)
+        make_identity(nc, ident[:])
+
+        def load_x(g):
+            nc.sync.dma_start(out=xw[g][:], in_=x_words[g].rearrange("p n t -> p (n t)").bitcast(I32))
+
+        def load_w(k, words):
+            nc.sync.dma_start(out=ww[k][:].bitcast(I32), in_=words.rearrange("g p n -> p g n").bitcast(I32))
+
+        nc.sync.dma_start(offs_t[:], offs)
+        load_x(0)
+        load_scales(nc.sync, xs, x_scales)
+        load_x(1)
+        load_w(0, w1_words)
+        load_scales(nc.sync, ws[0], w1_scales)
+        load_w(1, w2_words)
+        load_scales(nc.sync, ws[1], w2_scales)
+        nc.sync.dma_start(pb_t[:], pb)
+        nc.sync.dma_start(pa_t[:], pa)
+        nc.sync.dma_start(out=unit_t[:], in_=unit.rearrange("(p t) o -> p (t o)", t=4))
+        nc.sync.dma_start(out=w3w[:].bitcast(I32), in_=w3_words[0].bitcast(I32))
+        load_scales(nc.sync, w3s, w3_scales)
+        for t in range(4):
+            nc.sync.dma_start(out=ref_t[t][:], in_=ref[P * t : P * (t + 1), :])
+
+        xg = [sb("xg%d" % g, [P, S], U32) for g in range(PASSES)]
+        xgs = [sb("xgs%d" % g, [P, S], U8) for g in range(PASSES)]
+        for g in range(PASSES):
+            nc.vector.tensor_copy(xgs[g][:], xs[:, g, :].indirect(offs_t[:]))
+        for g in range(PASSES):
+            nc.vector.tensor_copy(xg[g][:], xw[g][:].bitcast(U32).indirect(offs_t[:]))
+
+        win = [[sb("win%d_%d" % (k, t), [P, S], F32) for t in range(4)] for k in range(2)]
+        first_banks = (4, 5, 6, 7, 3, 4, 5, 6)
+
+        def first_product(k, t):
+            acc = bank(first_banks[2 * t + k])
+            for g in range(PASSES):
+                nc.tensor.matmul_mx(
+                    out=acc[:],
+                    lhsT=ww[k][:, g, 2 * P * t : 2 * P * (t + 1)].bitcast(FP4X4),
+                    lhsT_scale=ws[k][:, g, P * t : P * (t + 1)],
+                    rhs=xg[g][:].bitcast(FP8X4),
+                    rhs_scale=xgs[g][:],
+                    start=(g == 0),
+                    stop=(g == PASSES - 1),
+                )
+            if (k, t) == (1, 0):
+                nc.vector.tensor_copy(win[k][t][:], acc[:])
+            else:
+                nc.scalar.copy(win[k][t][:], acc[:])
+
+        ubank = bank(0)
+        for t in range(4):
+            nc.tensor.matmul(
+                ubank[:, P * t : P * (t + 1)], unit_t[:, t : t + 1].to_broadcast([P, P]), ident[:],
+                start=True, stop=True, is_transpose=True,
+            )
+        unit_neg = sb("unit_neg", [P, 2, P, 2], F32)
+        nc.scalar.activation(
+            unit_neg[:], ubank[:].rearrange("r (u e p) -> r u p e", u=2, e=2), COPY, scale=-1.0
+        )
+
+        w3d = sb("w3d", [P, 4, P, 2], U8)
+        w3sd = sb("w3sd", [P, 4, P], U8)
+
+        def deal_w3():
+            nc.vector.tensor_copy(w3d[:], w3w[:].rearrange("k (m t b) -> k t m b", t=4, b=2))
+            nc.vector.tensor_copy(w3sd[:], w3s[:, 0, :].rearrange("k (m t) -> k t m", t=4))
+
+        oscale = sb("oscale", [P, U], U8)
+        out_rows = out_0.rearrange("(p t) r -> p t r", t=4)
+        out_words = out_1[0].rearrange("p r b -> p (r b)").bitcast(I32)
+
+        c0 = 0
+        blk = 0
+        for c, w in enumerate(CHUNKS):
+            nb = w // P
+            cols16 = slice(c0 // 16, (c0 + w) // 16)
+            accs = [bank((blk + j) % 4) for j in range(nb)] if c > 0 else None
+            for t in range(4):
+                if c == 0:
+                    first_product(0, t)
+                    first_product(1, t)
+                    if t == 0:
+                        deal_w3()
+                        accs = [bank(j) for j in range(nb)]
+                prods = []
+                for k in range(2):
+                    neg_b = keep.tile([P, w], F32, name="negb", tag="negb", bufs=4, align_bytes=64)
+                    nc.scalar.activation(neg_b[:], win[k][t][:].indirect(pb_t[:, cols16]), COPY, scale=-1.0)
+                    prod = keep.tile([P, w], F32, name="prod", tag="prod", bufs=4, align_bytes=64)
+                    nc.vector.tensor_tensor(prod[:], win[k][t][:].indirect(pa_t[:, cols16]), neg_b[:], MULT)
+                    prods.append(prod)
+                for j in range(nb):
+                    terms = (
+                        ref_t[t][:, c0 + P * j : c0 + P * (j + 1)],
+                        prods[0][:, P * j : P * (j + 1)],
+                        prods[1][:, P * j : P * (j + 1)],
+                    )
+                    for n, term in enumerate(terms):
+                        nc.tensor.matmul(
+                            accs[j][:, P * t : P * (t + 1)], term, ident[:],
+                            start=(n == 0), stop=(n == 2), is_transpose=True,
+                        )
+
+            hid = sb("hid%d" % c, [P, w, 4], BF16)
+            for j in range(nb):
+                hid_t = sb("hidT%d_%d" % (c, j), [P, 2, P, 2], BF16)
+                nc.vector.tensor_tensor(
+                    hid_t[:], accs[j][:].rearrange("r (p u e) -> r u p e", u=2, e=2), unit_neg[:], MULT
+                )
+                words = hid_t[:].rearrange("r u p e -> r (u p e)").bitcast(F32)
+                back = bank(4 + (blk + j) % 2)
+                for u in range(2):
+                    nc.tensor.transpose(back[:, P * u : P * (u + 1)], words[:, P * u : P * (u + 1)], ident[:])
+                nc.scalar.copy(
+                    hid[:, P * j : P * (j + 1), :].bitcast(F32),
+                    back[:, 0 : 2 * P].rearrange("p (u r) -> p r u", u=2),
+                )
+            hcode = sb("hcode%d" % c, [P, w], U32)
+            hscale = sb("hscale%d" % c, [P, w], U8)
+            nc.vector.quantize_mx(
+                out=hcode[:].bitcast(FP8X4), scales=hscale[:], in_=hid[:].rearrange("p r t -> p (r t)")
+            )
+            o32 = sb("o32_%d" % c, [P, 4, w], F32)
+            for j in range(nb):
+                ob = bank(6 + (blk + j) % 2)
+                for t in range(4):
+                    nc.tensor.matmul_mx(
+                        out=ob[:, P * t : P * (t + 1)],
+                        lhsT=w3d[:, t, :, :].rearrange("k m b -> k (m b)").bitcast(FP4X4),
+                        lhsT_scale=w3sd[:, t, :],
+                        rhs=hcode[:, P * j : P * (j + 1)].bitcast(FP8X4),
+                        rhs_scale=hscale[:, P * j : P * (j + 1)],
+                        start=True,
+                        stop=True,
+                    )
+                nc.scalar.copy(o32[:, :, P * j : P * (j + 1)], ob[:].rearrange("p (t r) -> p t r", t=4))
+            nc.sync.dma_start(out=out_rows[:, :, c0 : c0 + w], in_=o32[:])
+            obf = sb("obf%d" % c, [P, w, 4], BF16)
+            nc.vector.tensor_copy(obf[:], o32[:].rearrange("p t r -> p r t"))
+            ocode = sb("ocode%d" % c, [P, w], I32)
+            nc.vector.quantize_mx(
+                out=ocode[:].bitcast(FP8X4),
+                scales=oscale[:, c0 : c0 + w],
+                in_=obf[:].rearrange("p r t -> p (r t)"),
+            )
+            nc.sync.dma_start(out=out_words[:, c0 : c0 + w], in_=ocode[:])
+            c0 = c0 + w
+            blk = blk + nb
+
+        for q in range(4):
+            nc.sync.dma_start(
+                out=out_2[0, 4 * q : 4 * q + 4, :].bitcast(I32),
+                in_=oscale[32 * q : 32 * q + 4, :].bitcast(I32),
+            )

@@ -19,7 +19,8 @@ COPY = mybir.ActivationFunctionType.Copy
 
 P = 128
 PASSES = K // 512
-CHUNKS = (384, 256, 256, 128)
+CHUNKS = (512, 512)
+SPARE = 16
 
 
 def tile_picked_ycrossp_dot_po_kernel(
@@ -47,7 +48,7 @@ def tile_picked_ycrossp_dot_po_kernel(
         offs_t = sb("offs_t", [P, S // 16], U16)
         pa_t = sb("pa_t", [P, U // 16], U16)
         pb_t = sb("pb_t", [P, U // 16], U16)
-        xw = [sb("xw%d" % g, [P, T], I32) for g in range(PASSES)]
+        xw = sb("xw", [P, PASSES, T], I32)
         xs = sb("xs", [P, PASSES, T], U8)
         ww = [sb("ww%d" % k, [P, PASSES, 2 * H], U8) for k in range(2)]
         ws = [sb("ws%d" % k, [P, PASSES, H], U8) for k in range(2)]
@@ -57,29 +58,23 @@ def tile_picked_ycrossp_dot_po_kernel(
         ref_t = [sb("ref%d" % t, [P, U], F32) for t in range(4)]
         ident = sb("ident", [P, P], F32)
 
-        nc.vector.memset(xs[:].bitcast(I32), 0)
-        nc.gpsimd.memset(ws[0][:].bitcast(I32), 0)
-        nc.gpsimd.memset(ws[1][:].bitcast(I32), 0)
+        nc.gpsimd.memset(xs[:].bitcast(I32), 0)
         nc.gpsimd.memset(w3s[:].bitcast(I32), 0)
-        make_identity(nc, ident[:])
-
-        def load_x(g):
-            nc.sync.dma_start(out=xw[g][:], in_=x_words[g].rearrange("p n t -> p (n t)").bitcast(I32))
 
         def load_w(k, words):
             nc.sync.dma_start(out=ww[k][:].bitcast(I32), in_=words.rearrange("g p n -> p g n").bitcast(I32))
 
+        make_identity(nc, ident[:])
         nc.sync.dma_start(offs_t[:], offs)
-        load_x(0)
         load_scales(nc.sync, xs, x_scales)
-        load_x(1)
+        nc.sync.dma_start(out=unit_t[:], in_=unit.rearrange("(p t) o -> p (t o)", t=4))
+        nc.sync.dma_start(out=xw[:], in_=x_words.rearrange("g p n t -> p g (n t)").bitcast(I32))
         load_w(0, w1_words)
         load_scales(nc.sync, ws[0], w1_scales)
-        load_w(1, w2_words)
-        load_scales(nc.sync, ws[1], w2_scales)
         nc.sync.dma_start(pb_t[:], pb)
         nc.sync.dma_start(pa_t[:], pa)
-        nc.sync.dma_start(out=unit_t[:], in_=unit.rearrange("(p t) o -> p (t o)", t=4))
+        load_w(1, w2_words)
+        load_scales(nc.sync, ws[1], w2_scales)
         nc.sync.dma_start(out=w3w[:].bitcast(I32), in_=w3_words[0].bitcast(I32))
         load_scales(nc.sync, w3s, w3_scales)
         for t in range(4):
@@ -87,41 +82,50 @@ def tile_picked_ycrossp_dot_po_kernel(
 
         xg = [sb("xg%d" % g, [P, S], U32) for g in range(PASSES)]
         xgs = [sb("xgs%d" % g, [P, S], U8) for g in range(PASSES)]
+        win = [[sb("win%d_%d" % (k, t), [P, S + SPARE], F32) for t in range(4)] for k in range(2)]
+
         for g in range(PASSES):
             nc.vector.tensor_copy(xgs[g][:], xs[:, g, :].indirect(offs_t[:]))
         for g in range(PASSES):
-            nc.vector.tensor_copy(xg[g][:], xw[g][:].bitcast(U32).indirect(offs_t[:]))
+            nc.vector.tensor_copy(xg[g][:], xw[:, g, :].bitcast(U32).indirect(offs_t[:]))
 
-        win = [[sb("win%d_%d" % (k, t), [P, S], F32) for t in range(4)] for k in range(2)]
-        first_banks = (4, 5, 6, 7, 3, 4, 5, 6)
+        first_banks = ((0, 1), (2, 3), (1, 0), (3, 2))
 
-        def first_product(k, t):
-            acc = bank(first_banks[2 * t + k])
-            for g in range(PASSES):
-                nc.tensor.matmul_mx(
-                    out=acc[:],
-                    lhsT=ww[k][:, g, 2 * P * t : 2 * P * (t + 1)].bitcast(FP4X4),
-                    lhsT_scale=ws[k][:, g, P * t : P * (t + 1)],
-                    rhs=xg[g][:].bitcast(FP8X4),
-                    rhs_scale=xgs[g][:],
-                    start=(g == 0),
-                    stop=(g == PASSES - 1),
-                )
-            if (k, t) == (1, 0):
-                nc.vector.tensor_copy(win[k][t][:], acc[:])
-            else:
-                nc.scalar.copy(win[k][t][:], acc[:])
-
-        ubank = bank(0)
-        for t in range(4):
-            nc.tensor.matmul(
-                ubank[:, P * t : P * (t + 1)], unit_t[:, t : t + 1].to_broadcast([P, P]), ident[:],
-                start=True, stop=True, is_transpose=True,
+        def first_pass(acc, k, t, g):
+            nc.tensor.matmul_mx(
+                out=acc[:],
+                lhsT=ww[k][:, g, 2 * P * t : 2 * P * (t + 1)].bitcast(FP4X4),
+                lhsT_scale=ws[k][:, g, P * t : P * (t + 1)],
+                rhs=xg[g][:].bitcast(FP8X4),
+                rhs_scale=xgs[g][:],
+                start=(g == 0),
+                stop=(g == PASSES - 1),
             )
+
+        def first_products(ts):
+            pairs = [(k, t) for k in range(2) for t in ts]
+            accs = {pair: bank(first_banks[pair[1]][pair[0]]) for pair in pairs}
+            for k, t in pairs:
+                first_pass(accs[k, t], k, t, 0)
+            for k, t in pairs:
+                first_pass(accs[k, t], k, t, 1)
+                copy = nc.vector.tensor_copy if (k, t) in ((0, 1), (1, 0)) else nc.scalar.copy
+                copy(win[k][t][:, 0:S], accs[k, t][:])
+
         unit_neg = sb("unit_neg", [P, 2, P, 2], F32)
-        nc.scalar.activation(
-            unit_neg[:], ubank[:].rearrange("r (u e p) -> r u p e", u=2, e=2), COPY, scale=-1.0
-        )
+
+        def spread_unit():
+            ubank = bank(7)
+            for t in range(4):
+                nc.tensor.matmul(
+                    ubank[:, P * t : P * (t + 1)], unit_t[:, t : t + 1].to_broadcast([P, P]), ident[:],
+                    start=True, stop=True, is_transpose=True,
+                )
+            nc.scalar.activation(
+                unit_neg[:], ubank[:].rearrange("r (u e p) -> r u p e", u=2, e=2), COPY, scale=-1.0
+            )
+
+        spread_unit()
 
         w3d = sb("w3d", [P, 4, P, 2], U8)
         w3sd = sb("w3sd", [P, 4, P], U8)
@@ -134,19 +138,67 @@ def tile_picked_ycrossp_dot_po_kernel(
         out_rows = out_0.rearrange("(p t) r -> p t r", t=4)
         out_words = out_1[0].rearrange("p r b -> p (r b)").bitcast(I32)
 
+        def finish(accs, r0, w):
+            hid = sb("hid%d" % r0, [P, w, 4], BF16)
+            for j, acc in enumerate(accs):
+                hid_t = sb("hidT%d_%d" % (r0, j), [P, 2, P, 2], BF16)
+                nc.vector.tensor_tensor(
+                    hid_t[:], acc[:].rearrange("r (p u e) -> r u p e", u=2, e=2), unit_neg[:], MULT
+                )
+                words = hid_t[:].rearrange("r u p e -> r (u p e)").bitcast(F32)
+                back = bank((r0 // P + j) % 2)
+                for u in range(2):
+                    nc.tensor.transpose(back[:, P * u : P * (u + 1)], words[:, P * u : P * (u + 1)], ident[:])
+                nc.scalar.copy(
+                    hid[:, P * j : P * (j + 1), :].bitcast(F32),
+                    back[:, 0 : 2 * P].rearrange("p (u r) -> p r u", u=2),
+                )
+            hcode = sb("hcode%d" % r0, [P, w], U32)
+            hscale = sb("hscale%d" % r0, [P, w], U8)
+            nc.vector.quantize_mx(
+                out=hcode[:].bitcast(FP8X4), scales=hscale[:], in_=hid[:].rearrange("p r t -> p (r t)")
+            )
+            o32 = sb("o32_%d" % r0, [P, 4, w], F32)
+            obf = sb("obf%d" % r0, [P, w, 4], BF16)
+            from_psum = r0 in (512, 640)
+            for j in range(len(accs)):
+                ob = bank(2 + (r0 // P + j) % 2)
+                for t in range(4):
+                    nc.tensor.matmul_mx(
+                        out=ob[:, P * t : P * (t + 1)],
+                        lhsT=w3d[:, t, :, :].rearrange("k m b -> k (m b)").bitcast(FP4X4),
+                        lhsT_scale=w3sd[:, t, :],
+                        rhs=hcode[:, P * j : P * (j + 1)].bitcast(FP8X4),
+                        rhs_scale=hscale[:, P * j : P * (j + 1)],
+                        start=True,
+                        stop=True,
+                    )
+                nc.scalar.copy(o32[:, :, P * j : P * (j + 1)], ob[:].rearrange("p (t r) -> p t r", t=4))
+                if from_psum:
+                    nc.scalar.copy(obf[:], ob[:].rearrange("p (t r) -> p r t", t=4))
+            nc.sync.dma_start(out=out_rows[:, :, r0 : r0 + w], in_=o32[:])
+            if not from_psum:
+                nc.vector.tensor_copy(obf[:], o32[:].rearrange("p t r -> p r t"))
+            ocode = sb("ocode%d" % r0, [P, w], I32)
+            nc.vector.quantize_mx(
+                out=ocode[:].bitcast(FP8X4),
+                scales=oscale[:, r0 : r0 + w],
+                in_=obf[:].rearrange("p r t -> p (r t)"),
+            )
+            nc.sync.dma_start(out=out_words[:, r0 : r0 + w], in_=ocode[:])
+
         c0 = 0
         blk = 0
         for c, w in enumerate(CHUNKS):
             nb = w // P
             cols16 = slice(c0 // 16, (c0 + w) // 16)
-            accs = [bank((blk + j) % 4) for j in range(nb)] if c > 0 else None
+            accs = [bank(4 + (blk + j) % 4) for j in range(nb)]
             for t in range(4):
                 if c == 0:
-                    first_product(0, t)
-                    first_product(1, t)
-                    if t == 0:
+                    if t != 1:
+                        first_products((0, 1) if t == 0 else (t,))
+                    if t == 1:
                         deal_w3()
-                        accs = [bank(j) for j in range(nb)]
                 prods = []
                 for k in range(2):
                     neg_b = keep.tile([P, w], F32, name="negb", tag="negb", bufs=4, align_bytes=64)
@@ -166,49 +218,9 @@ def tile_picked_ycrossp_dot_po_kernel(
                             start=(n == 0), stop=(n == 2), is_transpose=True,
                         )
 
-            hid = sb("hid%d" % c, [P, w, 4], BF16)
-            for j in range(nb):
-                hid_t = sb("hidT%d_%d" % (c, j), [P, 2, P, 2], BF16)
-                nc.vector.tensor_tensor(
-                    hid_t[:], accs[j][:].rearrange("r (p u e) -> r u p e", u=2, e=2), unit_neg[:], MULT
-                )
-                words = hid_t[:].rearrange("r u p e -> r (u p e)").bitcast(F32)
-                back = bank(4 + (blk + j) % 2)
-                for u in range(2):
-                    nc.tensor.transpose(back[:, P * u : P * (u + 1)], words[:, P * u : P * (u + 1)], ident[:])
-                nc.scalar.copy(
-                    hid[:, P * j : P * (j + 1), :].bitcast(F32),
-                    back[:, 0 : 2 * P].rearrange("p (u r) -> p r u", u=2),
-                )
-            hcode = sb("hcode%d" % c, [P, w], U32)
-            hscale = sb("hscale%d" % c, [P, w], U8)
-            nc.vector.quantize_mx(
-                out=hcode[:].bitcast(FP8X4), scales=hscale[:], in_=hid[:].rearrange("p r t -> p (r t)")
-            )
-            o32 = sb("o32_%d" % c, [P, 4, w], F32)
-            for j in range(nb):
-                ob = bank(6 + (blk + j) % 2)
-                for t in range(4):
-                    nc.tensor.matmul_mx(
-                        out=ob[:, P * t : P * (t + 1)],
-                        lhsT=w3d[:, t, :, :].rearrange("k m b -> k (m b)").bitcast(FP4X4),
-                        lhsT_scale=w3sd[:, t, :],
-                        rhs=hcode[:, P * j : P * (j + 1)].bitcast(FP8X4),
-                        rhs_scale=hscale[:, P * j : P * (j + 1)],
-                        start=True,
-                        stop=True,
-                    )
-                nc.scalar.copy(o32[:, :, P * j : P * (j + 1)], ob[:].rearrange("p (t r) -> p t r", t=4))
-            nc.sync.dma_start(out=out_rows[:, :, c0 : c0 + w], in_=o32[:])
-            obf = sb("obf%d" % c, [P, w, 4], BF16)
-            nc.vector.tensor_copy(obf[:], o32[:].rearrange("p t r -> p r t"))
-            ocode = sb("ocode%d" % c, [P, w], I32)
-            nc.vector.quantize_mx(
-                out=ocode[:].bitcast(FP8X4),
-                scales=oscale[:, c0 : c0 + w],
-                in_=obf[:].rearrange("p r t -> p (r t)"),
-            )
-            nc.sync.dma_start(out=out_words[:, c0 : c0 + w], in_=ocode[:])
+            group = w if c == 0 else P
+            for g0 in range(0, w, group):
+                finish(accs[g0 // P : (g0 + group) // P], c0 + g0, group)
             c0 = c0 + w
             blk = blk + nb
 

@@ -18,9 +18,16 @@ MULT = mybir.AluOpType.mult
 COPY = mybir.ActivationFunctionType.Copy
 
 P = 128
-PASSES = K // 512
-CHUNKS = (512, 512)
-SPARE = 16
+PACK = 4
+PASSES = K // (P * PACK)
+TILES = H // P
+CHUNK = 512
+BLOCKS = CHUNK // P
+HALF = CHUNK // 2
+WINDOW = S + 16
+AHEAD = 4
+Z_ON_VECTOR = 3
+SUM_BANKS = (4, 5, 6, 7)
 
 
 def tile_picked_ycrossp_dot_po_kernel(
@@ -32,200 +39,242 @@ def tile_picked_ycrossp_dot_po_kernel(
         keep = ctx.enter_context(tc.tile_pool(name="keep", bufs=1))
         psum = ctx.enter_context(tc.psum_pool(name="psum", bufs=1))
 
-        def sb(name, shape, dtype):
-            return keep.tile(shape, dtype, name=name, align_bytes=64)
+        def sbuf(name, shape, dtype):
+            return keep.tile(shape, dtype, name=name, tag=name, align_bytes=64)
 
         def bank(b):
             return psum.tile([P, 512], F32, name="bank%d" % b, tag="bank%d" % b)
 
-        def load_scales(queue, plane, scales):
+        offs_t = sbuf("offs_t", [P, S // 16], U16)
+        pa_t = sbuf("pa_t", [P, U // 16], U16)
+        pb_t = sbuf("pb_t", [P, U // 16], U16)
+        x_w = sbuf("x_w", [P, PASSES, T], I32)
+        x_s = sbuf("x_s", [P, PASSES, T], U8)
+        w_w = [sbuf("w_w%d" % k, [P, PASSES, 2 * H], U8) for k in range(2)]
+        w_s = [sbuf("w_s%d" % k, [P, PASSES, H], U8) for k in range(2)]
+        w3_w = sbuf("w3_w", [P, 2 * N], U8)
+        w3_s = sbuf("w3_s", [P, 1, N], U8)
+        unit_t = sbuf("unit_t", [P, PACK], F32)
+        ref_t = [sbuf("ref%d" % t, [P, U], F32) for t in range(TILES)]
+        ident = sbuf("ident", [P, P], F32)
+
+        nc.gpsimd.memset(x_s[:].bitcast(I32), 0)
+        nc.gpsimd.memset(w3_s[:].bitcast(I32), 0)
+        make_identity(nc, ident[:])
+
+        def load_scales(plane, scales):
             for q in range(4):
-                queue.dma_start(
+                nc.sync.dma_start(
                     out=plane[32 * q : 32 * q + 4, :, :].bitcast(I32),
                     in_=scales[:, 4 * q : 4 * q + 4, :].rearrange("g q c -> q g c").bitcast(I32),
                 )
 
-        offs_t = sb("offs_t", [P, S // 16], U16)
-        pa_t = sb("pa_t", [P, U // 16], U16)
-        pb_t = sb("pb_t", [P, U // 16], U16)
-        xw = sb("xw", [P, PASSES, T], I32)
-        xs = sb("xs", [P, PASSES, T], U8)
-        ww = [sb("ww%d" % k, [P, PASSES, 2 * H], U8) for k in range(2)]
-        ws = [sb("ws%d" % k, [P, PASSES, H], U8) for k in range(2)]
-        w3w = sb("w3w", [P, 2 * N], U8)
-        w3s = sb("w3s", [P, 1, N], U8)
-        unit_t = sb("unit_t", [P, 4], F32)
-        ref_t = [sb("ref%d" % t, [P, U], F32) for t in range(4)]
-        ident = sb("ident", [P, P], F32)
+        def load_weight(k, words, scales):
+            nc.sync.dma_start(out=w_w[k][:].bitcast(I32), in_=words.rearrange("g p n -> p g n").bitcast(I32))
+            load_scales(w_s[k], scales)
 
-        nc.gpsimd.memset(xs[:].bitcast(I32), 0)
-        nc.gpsimd.memset(w3s[:].bitcast(I32), 0)
-
-        def load_w(k, words):
-            nc.sync.dma_start(out=ww[k][:].bitcast(I32), in_=words.rearrange("g p n -> p g n").bitcast(I32))
-
-        make_identity(nc, ident[:])
         nc.sync.dma_start(offs_t[:], offs)
-        load_scales(nc.sync, xs, x_scales)
-        nc.sync.dma_start(out=unit_t[:], in_=unit.rearrange("(p t) o -> p (t o)", t=4))
-        nc.sync.dma_start(out=xw[:], in_=x_words.rearrange("g p n t -> p g (n t)").bitcast(I32))
-        load_w(0, w1_words)
-        load_scales(nc.sync, ws[0], w1_scales)
+        load_scales(x_s, x_scales)
         nc.sync.dma_start(pb_t[:], pb)
+        nc.sync.dma_start(out=x_w[:], in_=x_words.rearrange("g p n t -> p g (n t)").bitcast(I32))
+        load_weight(0, w1_words, w1_scales)
+        nc.sync.dma_start(out=unit_t[:], in_=unit.rearrange("(p t) o -> p (t o)", t=PACK))
+        load_weight(1, w2_words, w2_scales)
+        nc.sync.dma_start(out=w3_w[:].bitcast(I32), in_=w3_words[0].bitcast(I32))
+        load_scales(w3_s, w3_scales)
         nc.sync.dma_start(pa_t[:], pa)
-        load_w(1, w2_words)
-        load_scales(nc.sync, ws[1], w2_scales)
-        nc.sync.dma_start(out=w3w[:].bitcast(I32), in_=w3_words[0].bitcast(I32))
-        load_scales(nc.sync, w3s, w3_scales)
-        for t in range(4):
+        for t in range(TILES):
             nc.sync.dma_start(out=ref_t[t][:], in_=ref[P * t : P * (t + 1), :])
 
-        xg = [sb("xg%d" % g, [P, S], U32) for g in range(PASSES)]
-        xgs = [sb("xgs%d" % g, [P, S], U8) for g in range(PASSES)]
-        win = [[sb("win%d_%d" % (k, t), [P, S + SPARE], F32) for t in range(4)] for k in range(2)]
-
+        picked_w = [sbuf("picked_w%d" % g, [P, S], U32) for g in range(PASSES)]
+        picked_s = [sbuf("picked_s%d" % g, [P, S], U8) for g in range(PASSES)]
         for g in range(PASSES):
-            nc.vector.tensor_copy(xgs[g][:], xs[:, g, :].indirect(offs_t[:]))
+            nc.vector.tensor_copy(picked_s[g][:], x_s[:, g, :].indirect(offs_t[:]))
         for g in range(PASSES):
-            nc.vector.tensor_copy(xg[g][:], xw[:, g, :].bitcast(U32).indirect(offs_t[:]))
+            nc.vector.tensor_copy(picked_w[g][:], x_w[:, g, :].bitcast(U32).indirect(offs_t[:]))
 
-        first_banks = ((0, 1), (2, 3), (1, 0), (3, 2))
+        win = [[sbuf("win%d_%d" % (k, t), [P, WINDOW], F32) for t in range(TILES)] for k in range(2)]
 
-        def first_pass(acc, k, t, g):
-            nc.tensor.matmul_mx(
-                out=acc[:],
-                lhsT=ww[k][:, g, 2 * P * t : 2 * P * (t + 1)].bitcast(FP4X4),
-                lhsT_scale=ws[k][:, g, P * t : P * (t + 1)],
-                rhs=xg[g][:].bitcast(FP8X4),
-                rhs_scale=xgs[g][:],
-                start=(g == 0),
-                stop=(g == PASSES - 1),
-            )
+        def first_products(t):
+            accs = [bank((t + k) % 3) for k in range(2)]
 
-        def first_products(ts):
-            pairs = [(k, t) for k in range(2) for t in ts]
-            accs = {pair: bank(first_banks[pair[1]][pair[0]]) for pair in pairs}
-            for k, t in pairs:
-                first_pass(accs[k, t], k, t, 0)
-            for k, t in pairs:
-                first_pass(accs[k, t], k, t, 1)
-                copy = nc.vector.tensor_copy if (k, t) in ((0, 1), (1, 0)) else nc.scalar.copy
-                copy(win[k][t][:, 0:S], accs[k, t][:])
-
-        unit_neg = sb("unit_neg", [P, 2, P, 2], F32)
-
-        def spread_unit():
-            ubank = bank(7)
-            for t in range(4):
-                nc.tensor.matmul(
-                    ubank[:, P * t : P * (t + 1)], unit_t[:, t : t + 1].to_broadcast([P, P]), ident[:],
-                    start=True, stop=True, is_transpose=True,
+            def one_pass(k, g):
+                nc.tensor.matmul_mx(
+                    out=accs[k][:],
+                    lhsT=w_w[k][:, g, 2 * P * t : 2 * P * (t + 1)].bitcast(FP4X4),
+                    lhsT_scale=w_s[k][:, g, P * t : P * (t + 1)],
+                    rhs=picked_w[g][:].bitcast(FP8X4),
+                    rhs_scale=picked_s[g][:],
+                    start=(g == 0),
+                    stop=(g == PASSES - 1),
                 )
-            nc.scalar.activation(
-                unit_neg[:], ubank[:].rearrange("r (u e p) -> r u p e", u=2, e=2), COPY, scale=-1.0
+
+            for k in range(2):
+                for g in range(PASSES):
+                    one_pass(k, g)
+                copy = nc.vector.tensor_copy if k == 1 and t < Z_ON_VECTOR else nc.scalar.copy
+                copy(win[k][t][:, 0:S], accs[k][:])
+
+        unit_bank = bank(SUM_BANKS[-1])
+        for t in range(PACK):
+            nc.tensor.matmul(
+                unit_bank[:, P * t : P * (t + 1)], unit_t[:, t : t + 1].to_broadcast([P, P]), ident[:],
+                start=True, stop=True, is_transpose=True,
             )
+        unit_neg = sbuf("unit_neg", [P, 2, P, 2], F32)
+        nc.scalar.activation(
+            unit_neg[:], unit_bank[:].rearrange("r (u e p) -> r u p e", u=2, e=2), COPY, scale=-1.0
+        )
 
-        spread_unit()
-
-        w3d = sb("w3d", [P, 4, P, 2], U8)
-        w3sd = sb("w3sd", [P, 4, P], U8)
+        dealt_w = sbuf("dealt_w", [P, PACK, P, 2], U8)
+        dealt_s = sbuf("dealt_s", [P, PACK, P], U8)
 
         def deal_w3():
-            nc.vector.tensor_copy(w3d[:], w3w[:].rearrange("k (m t b) -> k t m b", t=4, b=2))
-            nc.vector.tensor_copy(w3sd[:], w3s[:, 0, :].rearrange("k (m t) -> k t m", t=4))
+            nc.vector.tensor_copy(dealt_w[:], w3_w[:].rearrange("k (j t b) -> k t j b", t=PACK, b=2))
+            nc.vector.tensor_copy(dealt_s[:], w3_s[:, 0, :].rearrange("k (j t) -> k t j", t=PACK))
 
-        oscale = sb("oscale", [P, U], U8)
-        out_rows = out_0.rearrange("(p t) r -> p t r", t=4)
-        out_words = out_1[0].rearrange("p r b -> p (r b)").bitcast(I32)
+        prods = {}
 
-        def finish(accs, r0, w):
-            hid = sb("hid%d" % r0, [P, w, 4], BF16)
-            for j, acc in enumerate(accs):
-                hid_t = sb("hidT%d_%d" % (r0, j), [P, 2, P, 2], BF16)
+        def look_up(c, t, k, buffer=None, pieces=1):
+            n = 2 * (TILES * c + t) + k
+            neg_b = sbuf("neg_b%d" % (n % AHEAD), [P, CHUNK], F32)
+            r0 = c * CHUNK
+            nc.scalar.activation(
+                neg_b[:], win[k][t][:].indirect(pb_t[:, r0 // 16 : (r0 + CHUNK) // 16]), COPY, scale=-1.0
+            )
+            prod = sbuf(buffer or "prod%d" % n, [P, CHUNK], F32)
+            width = CHUNK // pieces
+            for lo in range(0, CHUNK, width):
+                nc.vector.tensor_tensor(
+                    prod[:, lo : lo + width],
+                    win[k][t][:].indirect(pa_t[:, (r0 + lo) // 16 : (r0 + lo + width) // 16]),
+                    neg_b[:, lo : lo + width],
+                    MULT,
+                )
+            prods[c, t, k] = prod
+
+        def add_up(sums, c, t):
+            for j in range(BLOCKS):
+                terms = (
+                    ref_t[t][:, c * CHUNK + P * j : c * CHUNK + P * (j + 1)],
+                    prods[c, t, 0][:, P * j : P * (j + 1)],
+                    prods[c, t, 1][:, P * j : P * (j + 1)],
+                )
+                for n, term in enumerate(terms):
+                    nc.tensor.matmul(
+                        sums[j][:, P * t : P * (t + 1)], term, ident[:],
+                        start=(n == 0), stop=(n == len(terms) - 1), is_transpose=True,
+                    )
+
+        def rounded(sums, r0, back_banks):
+            hid = sbuf("hid%d" % r0, [P, P * len(sums), PACK], BF16)
+            for j, acc in enumerate(sums):
+                hid_t = sbuf("hid_t%d" % (r0 + P * j), [P, 2, P, 2], BF16)
                 nc.vector.tensor_tensor(
                     hid_t[:], acc[:].rearrange("r (p u e) -> r u p e", u=2, e=2), unit_neg[:], MULT
                 )
                 words = hid_t[:].rearrange("r u p e -> r (u p e)").bitcast(F32)
-                back = bank((r0 // P + j) % 2)
+                back = bank(back_banks[(r0 // P + j) % len(back_banks)])
                 for u in range(2):
                     nc.tensor.transpose(back[:, P * u : P * (u + 1)], words[:, P * u : P * (u + 1)], ident[:])
                 nc.scalar.copy(
                     hid[:, P * j : P * (j + 1), :].bitcast(F32),
                     back[:, 0 : 2 * P].rearrange("p (u r) -> p r u", u=2),
                 )
-            hcode = sb("hcode%d" % r0, [P, w], U32)
-            hscale = sb("hscale%d" % r0, [P, w], U8)
+            return hid
+
+        def quantised(hid, r0):
+            width = hid.shape[1]
+            codes = sbuf("hid_codes%d" % r0, [P, width], U32)
+            scales = sbuf("hid_scales%d" % r0, [P, width], U8)
             nc.vector.quantize_mx(
-                out=hcode[:].bitcast(FP8X4), scales=hscale[:], in_=hid[:].rearrange("p r t -> p (r t)")
+                out=codes[:].bitcast(FP8X4), scales=scales[:], in_=hid[:].rearrange("p r t -> p (r t)")
             )
-            o32 = sb("o32_%d" % r0, [P, 4, w], F32)
-            obf = sb("obf%d" % r0, [P, w, 4], BF16)
-            from_psum = r0 in (512, 640)
-            for j in range(len(accs)):
-                ob = bank(2 + (r0 // P + j) % 2)
-                for t in range(4):
+            return codes, scales
+
+        out_rows = out_0.rearrange("(p t) r -> p t r", t=PACK)
+        out_words = out_1[0].rearrange("p r b -> p (r b)").bitcast(I32)
+        out_codes = sbuf("out_codes", [P, U], I32)
+        out_scales = sbuf("out_scales", [P, U], U8)
+
+        def result(codes, scales, r0, out_banks, scalar_rounds):
+            width = codes.shape[1]
+            out_f = sbuf("out_f%d" % r0, [P, PACK, width], F32)
+            out_b = sbuf("out_b%d" % r0, [P, width, PACK], BF16)
+            for j in range(width // P):
+                cols = slice(P * j, P * (j + 1))
+                acc = bank(out_banks[j])
+                for t in range(PACK):
                     nc.tensor.matmul_mx(
-                        out=ob[:, P * t : P * (t + 1)],
-                        lhsT=w3d[:, t, :, :].rearrange("k m b -> k (m b)").bitcast(FP4X4),
-                        lhsT_scale=w3sd[:, t, :],
-                        rhs=hcode[:, P * j : P * (j + 1)].bitcast(FP8X4),
-                        rhs_scale=hscale[:, P * j : P * (j + 1)],
+                        out=acc[:, P * t : P * (t + 1)],
+                        lhsT=dealt_w[:, t, :, :].rearrange("k j b -> k (j b)").bitcast(FP4X4),
+                        lhsT_scale=dealt_s[:, t, :],
+                        rhs=codes[:, cols].bitcast(FP8X4),
+                        rhs_scale=scales[:, cols],
                         start=True,
                         stop=True,
                     )
-                nc.scalar.copy(o32[:, :, P * j : P * (j + 1)], ob[:].rearrange("p (t r) -> p t r", t=4))
-                if from_psum:
-                    nc.scalar.copy(obf[:], ob[:].rearrange("p (t r) -> p r t", t=4))
-            nc.sync.dma_start(out=out_rows[:, :, r0 : r0 + w], in_=o32[:])
-            if not from_psum:
-                nc.vector.tensor_copy(obf[:], o32[:].rearrange("p t r -> p r t"))
-            ocode = sb("ocode%d" % r0, [P, w], I32)
+                nc.scalar.copy(out_f[:, :, cols], acc[:].rearrange("p (t r) -> p t r", t=PACK))
+                if scalar_rounds:
+                    nc.scalar.copy(out_b[:, cols, :], acc[:].rearrange("p (t r) -> p r t", t=PACK))
+            nc.sync.dma_start(out=out_rows[:, :, r0 : r0 + width], in_=out_f[:])
+            if not scalar_rounds:
+                nc.vector.tensor_copy(out_b[:], out_f[:].rearrange("p t r -> p r t"))
+            return out_b
+
+        def planes(out_b, r0):
+            width = out_b.shape[1]
             nc.vector.quantize_mx(
-                out=ocode[:].bitcast(FP8X4),
-                scales=oscale[:, r0 : r0 + w],
-                in_=obf[:].rearrange("p r t -> p (r t)"),
+                out=out_codes[:, r0 : r0 + width].bitcast(FP8X4),
+                scales=out_scales[:, r0 : r0 + width],
+                in_=out_b[:].rearrange("p r t -> p (r t)"),
             )
-            nc.sync.dma_start(out=out_words[:, r0 : r0 + w], in_=ocode[:])
 
-        c0 = 0
-        blk = 0
-        for c, w in enumerate(CHUNKS):
-            nb = w // P
-            cols16 = slice(c0 // 16, (c0 + w) // 16)
-            accs = [bank(4 + (blk + j) % 4) for j in range(nb)]
-            for t in range(4):
-                if c == 0:
-                    if t != 1:
-                        first_products((0, 1) if t == 0 else (t,))
-                    if t == 1:
-                        deal_w3()
-                prods = []
-                for k in range(2):
-                    neg_b = keep.tile([P, w], F32, name="negb", tag="negb", bufs=4, align_bytes=64)
-                    nc.scalar.activation(neg_b[:], win[k][t][:].indirect(pb_t[:, cols16]), COPY, scale=-1.0)
-                    prod = keep.tile([P, w], F32, name="prod", tag="prod", bufs=4, align_bytes=64)
-                    nc.vector.tensor_tensor(prod[:], win[k][t][:].indirect(pa_t[:, cols16]), neg_b[:], MULT)
-                    prods.append(prod)
-                for j in range(nb):
-                    terms = (
-                        ref_t[t][:, c0 + P * j : c0 + P * (j + 1)],
-                        prods[0][:, P * j : P * (j + 1)],
-                        prods[1][:, P * j : P * (j + 1)],
-                    )
-                    for n, term in enumerate(terms):
-                        nc.tensor.matmul(
-                            accs[j][:, P * t : P * (t + 1)], term, ident[:],
-                            start=(n == 0), stop=(n == 2), is_transpose=True,
-                        )
+        def store_codes(r0, r1):
+            nc.sync.dma_start(out=out_words[:, r0:r1], in_=out_codes[:, r0:r1])
 
-            group = w if c == 0 else P
-            for g0 in range(0, w, group):
-                finish(accs[g0 // P : (g0 + group) // P], c0 + g0, group)
-            c0 = c0 + w
-            blk = blk + nb
+        sums = [bank(b) for b in SUM_BANKS]
+        for t in range(TILES):
+            first_products(t)
+            if t == 0:
+                deal_w3()
+            look_up(0, t, 0)
+            look_up(0, t, 1)
+            add_up(sums, 0, t)
+
+        look_up(1, 0, 0)
+        look_up(1, 0, 1)
+        halves = [quantised(rounded(sums[2 * h : 2 * h + 2], HALF * h, (0, 1)), HALF * h) for h in range(2)]
+        sums = [bank(b) for b in SUM_BANKS]
+        add_up(sums, 1, 0)
+        look_up(1, 1, 0, buffer="hid_t%d" % P)
+        look_up(1, 1, 1)
+        add_up(sums, 1, 1)
+        look_up(1, 2, 0)
+        look_up(1, 2, 1)
+        first_out = [result(*halves[0], 0, (2, 3), True)]
+        add_up(sums, 1, 2)
+        look_up(1, 3, 0)
+        look_up(1, 3, 1, pieces=2)
+        first_out.append(result(*halves[1], HALF, (2, 3), True))
+        add_up(sums, 1, 3)
+
+        starts = [CHUNK + P * j for j in range(BLOCKS)]
+        hids = [rounded(sums[j : j + 1], starts[j], (0, 1, 2, 3)) for j in range(BLOCKS)]
+        blocks = [quantised(hids[j], starts[j]) for j in range(BLOCKS)]
+        for h in range(2):
+            planes(first_out[h], HALF * h)
+        store_codes(0, CHUNK)
+        for j in range(BLOCKS):
+            last = j == BLOCKS - 1
+            planes(result(*blocks[j], starts[j], SUM_BANKS[j : j + 1], last), starts[j])
+            if j == BLOCKS - 2:
+                store_codes(CHUNK, starts[-1])
+        store_codes(starts[-1], U)
 
         for q in range(4):
-            nc.sync.dma_start(
+            queue = nc.sync if q % 2 else nc.scalar
+            queue.dma_start(
                 out=out_2[0, 4 * q : 4 * q + 4, :].bitcast(I32),
-                in_=oscale[32 * q : 32 * q + 4, :].bitcast(I32),
+                in_=out_scales[32 * q : 32 * q + 4, :].bitcast(I32),
             )

@@ -26,7 +26,7 @@ BLOCKS = CHUNK // P
 HALF = CHUNK // 2
 WINDOW = S + 16
 AHEAD = 4
-Z_ON_VECTOR = 3
+ON_VECTOR = 4
 SUM_BANKS = (4, 5, 6, 7)
 
 
@@ -48,7 +48,7 @@ def tile_picked_ycrossp_dot_po_kernel(
         offs_t = sbuf("offs_t", [P, S // 16], U16)
         pa_t = sbuf("pa_t", [P, U // 16], U16)
         pb_t = sbuf("pb_t", [P, U // 16], U16)
-        x_w = sbuf("x_w", [P, PASSES, T], I32)
+        x_w = [sbuf("x_w%d" % g, [P, T], I32) for g in range(PASSES)]
         x_s = sbuf("x_s", [P, PASSES, T], U8)
         w_w = [sbuf("w_w%d" % k, [P, PASSES, 2 * H], U8) for k in range(2)]
         w_s = [sbuf("w_s%d" % k, [P, PASSES, H], U8) for k in range(2)]
@@ -73,11 +73,15 @@ def tile_picked_ycrossp_dot_po_kernel(
             nc.sync.dma_start(out=w_w[k][:].bitcast(I32), in_=words.rearrange("g p n -> p g n").bitcast(I32))
             load_scales(w_s[k], scales)
 
+        def load_words(g):
+            nc.sync.dma_start(out=x_w[g][:], in_=x_words[g].rearrange("p n t -> p (n t)").bitcast(I32))
+
         nc.sync.dma_start(offs_t[:], offs)
+        load_words(0)
         load_scales(x_s, x_scales)
-        nc.sync.dma_start(pb_t[:], pb)
-        nc.sync.dma_start(out=x_w[:], in_=x_words.rearrange("g p n t -> p g (n t)").bitcast(I32))
+        load_words(1)
         load_weight(0, w1_words, w1_scales)
+        nc.sync.dma_start(pb_t[:], pb)
         nc.sync.dma_start(out=unit_t[:], in_=unit.rearrange("(p t) o -> p (t o)", t=PACK))
         load_weight(1, w2_words, w2_scales)
         nc.sync.dma_start(out=w3_w[:].bitcast(I32), in_=w3_words[0].bitcast(I32))
@@ -88,32 +92,41 @@ def tile_picked_ycrossp_dot_po_kernel(
 
         picked_w = [sbuf("picked_w%d" % g, [P, S], U32) for g in range(PASSES)]
         picked_s = [sbuf("picked_s%d" % g, [P, S], U8) for g in range(PASSES)]
+        nc.vector.tensor_copy(picked_w[0][:], x_w[0][:].bitcast(U32).indirect(offs_t[:]))
         for g in range(PASSES):
             nc.vector.tensor_copy(picked_s[g][:], x_s[:, g, :].indirect(offs_t[:]))
-        for g in range(PASSES):
-            nc.vector.tensor_copy(picked_w[g][:], x_w[:, g, :].bitcast(U32).indirect(offs_t[:]))
+        nc.vector.tensor_copy(picked_w[1][:], x_w[1][:].bitcast(U32).indirect(offs_t[:]))
 
         win = [[sbuf("win%d_%d" % (k, t), [P, WINDOW], F32) for t in range(TILES)] for k in range(2)]
 
-        def first_products(t):
-            accs = [bank((t + k) % 3) for k in range(2)]
+        def one_pass(acc, k, t, g):
+            nc.tensor.matmul_mx(
+                out=acc[:],
+                lhsT=w_w[k][:, g, 2 * P * t : 2 * P * (t + 1)].bitcast(FP4X4),
+                lhsT_scale=w_s[k][:, g, P * t : P * (t + 1)],
+                rhs=picked_w[g][:].bitcast(FP8X4),
+                rhs_scale=picked_s[g][:],
+                start=(g == 0),
+                stop=(g == PASSES - 1),
+            )
 
-            def one_pass(k, g):
-                nc.tensor.matmul_mx(
-                    out=accs[k][:],
-                    lhsT=w_w[k][:, g, 2 * P * t : 2 * P * (t + 1)].bitcast(FP4X4),
-                    lhsT_scale=w_s[k][:, g, P * t : P * (t + 1)],
-                    rhs=picked_w[g][:].bitcast(FP8X4),
-                    rhs_scale=picked_s[g][:],
-                    start=(g == 0),
-                    stop=(g == PASSES - 1),
-                )
+        def empty(acc, k, t):
+            copy = nc.vector.tensor_copy if 1 <= TILES * k + t <= ON_VECTOR else nc.scalar.copy
+            copy(win[k][t][:, 0:S], acc[:])
 
-            for k in range(2):
-                for g in range(PASSES):
-                    one_pass(k, g)
-                copy = nc.vector.tensor_copy if k == 1 and t < Z_ON_VECTOR else nc.scalar.copy
-                copy(win[k][t][:, 0:S], accs[k][:])
+        def y_products():
+            accs = [bank(t) for t in range(TILES)]
+            for t in range(TILES):
+                one_pass(accs[t], 0, t, 0)
+            for t in range(TILES):
+                one_pass(accs[t], 0, t, 1)
+                empty(accs[t], 0, t)
+
+        def z_product(t):
+            acc = bank(t)
+            for g in range(PASSES):
+                one_pass(acc, 1, t, g)
+            empty(acc, 1, t)
 
         unit_bank = bank(SUM_BANKS[-1])
         for t in range(PACK):
@@ -234,8 +247,9 @@ def tile_picked_ycrossp_dot_po_kernel(
             nc.sync.dma_start(out=out_words[:, r0:r1], in_=out_codes[:, r0:r1])
 
         sums = [bank(b) for b in SUM_BANKS]
+        y_products()
         for t in range(TILES):
-            first_products(t)
+            z_product(t)
             if t == 0:
                 deal_w3()
             look_up(0, t, 0)
@@ -247,11 +261,11 @@ def tile_picked_ycrossp_dot_po_kernel(
         halves = [quantised(rounded(sums[2 * h : 2 * h + 2], HALF * h, (0, 1)), HALF * h) for h in range(2)]
         sums = [bank(b) for b in SUM_BANKS]
         add_up(sums, 1, 0)
-        look_up(1, 1, 0, buffer="hid_t%d" % P)
-        look_up(1, 1, 1)
+        look_up(1, 1, 0, buffer="hid_t0")
+        look_up(1, 1, 1, buffer="hid_t%d" % P)
         add_up(sums, 1, 1)
-        look_up(1, 2, 0)
-        look_up(1, 2, 1)
+        look_up(1, 2, 0, buffer="hid_t%d" % (2 * P))
+        look_up(1, 2, 1, buffer="hid_t%d" % (3 * P))
         first_out = [result(*halves[0], 0, (2, 3), True)]
         add_up(sums, 1, 2)
         look_up(1, 3, 0)

from contextlib import ExitStack

import concourse.mybir as mybir
from concourse.masks import make_identity

K, T, S, H, N, U = 1024, 1024, 512, 512, 512, 1024
FLOPS = 2 * K * H * S * 2 + 2 * H * N * U

F32 = mybir.dt.float32
BF16 = mybir.dt.bfloat16
I32 = mybir.dt.int32
U32 = mybir.dt.uint32
U16 = mybir.dt.uint16
U8 = mybir.dt.uint8
FP8X4 = mybir.dt.float8_e4m3fn_x4
FP4X4 = mybir.dt.float4_e2m1fn_x4
MULT = mybir.AluOpType.mult
COPY = mybir.ActivationFunctionType.Copy

P = 128
PACK = 4
PASSES = K // (P * PACK)
TILES = H // P
CHUNK = 512
BLOCKS = CHUNK // P
HALF = CHUNK // 2
WINDOW = S + 16
AHEAD = 4
ON_VECTOR = 4
SUM_BANKS = (4, 5, 6, 7)


def tile_picked_ycrossp_dot_po_kernel(
    tc, x_words, x_scales, w1_words, w1_scales, w2_words, w2_scales, ref, unit,
    w3_words, w3_scales, offs, pa, pb, out_0, out_1, out_2,
):
    nc = tc.nc
    with ExitStack() as ctx:
        keep = ctx.enter_context(tc.tile_pool(name="keep", bufs=1))
        psum = ctx.enter_context(tc.psum_pool(name="psum", bufs=1))

        def sbuf(name, shape, dtype):
            return keep.tile(shape, dtype, name=name, tag=name, align_bytes=64)

        def bank(b):
            return psum.tile([P, 512], F32, name="bank%d" % b, tag="bank%d" % b)

        offs_t = sbuf("offs_t", [P, S // 16], U16)
        pa_t = sbuf("pa_t", [P, U // 16], U16)
        pb_t = sbuf("pb_t", [P, U // 16], U16)
        x_w = [sbuf("x_w%d" % g, [P, T], I32) for g in range(PASSES)]
        x_s = sbuf("x_s", [P, PASSES, T], U8)
        w_w = [sbuf("w_w%d" % k, [P, PASSES, 2 * H], U8) for k in range(2)]
        w_s = [sbuf("w_s%d" % k, [P, PASSES, H], U8) for k in range(2)]
        w3_w = sbuf("w3_w", [P, 2 * N], U8)
        w3_s = sbuf("w3_s", [P, 1, N], U8)
        unit_t = sbuf("unit_t", [P, PACK], F32)
        ref_t = [sbuf("ref%d" % t, [P, U], F32) for t in range(TILES)]
        ident = sbuf("ident", [P, P], F32)

        nc.gpsimd.memset(x_s[:].bitcast(I32), 0)
        nc.gpsimd.memset(w3_s[:].bitcast(I32), 0)
        make_identity(nc, ident[:])

        def load_scales(plane, scales):
            for q in range(4):
                nc.sync.dma_start(
                    out=plane[32 * q : 32 * q + 4, :, :].bitcast(I32),
                    in_=scales[:, 4 * q : 4 * q + 4, :].rearrange("g q c -> q g c").bitcast(I32),
                )

        def load_weight(k, words, scales):
            nc.sync.dma_start(out=w_w[k][:].bitcast(I32), in_=words.rearrange("g p n -> p g n").bitcast(I32))
            load_scales(w_s[k], scales)

        def load_words(g):
            nc.sync.dma_start(out=x_w[g][:], in_=x_words[g].rearrange("p n t -> p (n t)").bitcast(I32))

        nc.sync.dma_start(offs_t[:], offs)
        load_words(0)
        load_scales(x_s, x_scales)
        load_words(1)
        load_weight(0, w1_words, w1_scales)
        nc.sync.dma_start(pb_t[:], pb)
        nc.sync.dma_start(out=unit_t[:], in_=unit.rearrange("(p t) o -> p (t o)", t=PACK))
        load_weight(1, w2_words, w2_scales)
        nc.sync.dma_start(out=w3_w[:].bitcast(I32), in_=w3_words[0].bitcast(I32))
        load_scales(w3_s, w3_scales)
        nc.sync.dma_start(pa_t[:], pa)
        for t in range(TILES):
            nc.sync.dma_start(out=ref_t[t][:], in_=ref[P * t : P * (t + 1), :])

        picked_w = [sbuf("picked_w%d" % g, [P, S], U32) for g in range(PASSES)]
        picked_s = [sbuf("picked_s%d" % g, [P, S], U8) for g in range(PASSES)]
        nc.vector.tensor_copy(picked_w[0][:], x_w[0][:].bitcast(U32).indirect(offs_t[:]))
        for g in range(PASSES):
            nc.vector.tensor_copy(picked_s[g][:], x_s[:, g, :].indirect(offs_t[:]))
        nc.vector.tensor_copy(picked_w[1][:], x_w[1][:].bitcast(U32).indirect(offs_t[:]))

        win = [[sbuf("win%d_%d" % (k, t), [P, WINDOW], F32) for t in range(TILES)] for k in range(2)]

        def one_pass(acc, k, t, g):
            nc.tensor.matmul_mx(
                out=acc[:],
                lhsT=w_w[k][:, g, 2 * P * t : 2 * P * (t + 1)].bitcast(FP4X4),
                lhsT_scale=w_s[k][:, g, P * t : P * (t + 1)],
                rhs=picked_w[g][:].bitcast(FP8X4),
                rhs_scale=picked_s[g][:],
                start=(g == 0),
                stop=(g == PASSES - 1),
            )

        def empty(acc, k, t):
            copy = nc.vector.tensor_copy if 1 <= TILES * k + t <= ON_VECTOR else nc.scalar.copy
            copy(win[k][t][:, 0:S], acc[:])

        def y_products():
            accs = [bank(t) for t in range(TILES)]
            for t in range(TILES):
                one_pass(accs[t], 0, t, 0)
            for t in range(TILES):
                one_pass(accs[t], 0, t, 1)
                empty(accs[t], 0, t)

        def z_product(t):
            acc = bank(t)
            for g in range(PASSES):
                one_pass(acc, 1, t, g)
            empty(acc, 1, t)

        unit_bank = bank(SUM_BANKS[-1])
        for t in range(PACK):
            nc.tensor.matmul(
                unit_bank[:, P * t : P * (t + 1)], unit_t[:, t : t + 1].to_broadcast([P, P]), ident[:],
                start=True, stop=True, is_transpose=True,
            )
        unit_neg = sbuf("unit_neg", [P, 2, P, 2], F32)
        nc.scalar.activation(
            unit_neg[:], unit_bank[:].rearrange("r (u e p) -> r u p e", u=2, e=2), COPY, scale=-1.0
        )

        dealt_w = sbuf("dealt_w", [P, PACK, P, 2], U8)
        dealt_s = sbuf("dealt_s", [P, PACK, P], U8)

        def deal_w3():
            nc.vector.tensor_copy(dealt_w[:], w3_w[:].rearrange("k (j t b) -> k t j b", t=PACK, b=2))
            nc.vector.tensor_copy(dealt_s[:], w3_s[:, 0, :].rearrange("k (j t) -> k t j", t=PACK))

        prods = {}

        def look_up(c, t, k, buffer=None, pieces=1):
            n = 2 * (TILES * c + t) + k
            neg_b = sbuf("neg_b%d" % (n % AHEAD), [P, CHUNK], F32)
            r0 = c * CHUNK
            nc.scalar.activation(
                neg_b[:], win[k][t][:].indirect(pb_t[:, r0 // 16 : (r0 + CHUNK) // 16]), COPY, scale=-1.0
            )
            prod = sbuf(buffer or "prod%d" % n, [P, CHUNK], F32)
            width = CHUNK // pieces
            for lo in range(0, CHUNK, width):
                nc.vector.tensor_tensor(
                    prod[:, lo : lo + width],
                    win[k][t][:].indirect(pa_t[:, (r0 + lo) // 16 : (r0 + lo + width) // 16]),
                    neg_b[:, lo : lo + width],
                    MULT,
                )
            prods[c, t, k] = prod

        def add_up(sums, c, t):
            for j in range(BLOCKS):
                terms = (
                    ref_t[t][:, c * CHUNK + P * j : c * CHUNK + P * (j + 1)],
                    prods[c, t, 0][:, P * j : P * (j + 1)],
                    prods[c, t, 1][:, P * j : P * (j + 1)],
                )
                for n, term in enumerate(terms):
                    nc.tensor.matmul(
                        sums[j][:, P * t : P * (t + 1)], term, ident[:],
                        start=(n == 0), stop=(n == len(terms) - 1), is_transpose=True,
                    )

        def rounded(sums, r0, back_banks):
            hid = sbuf("hid%d" % r0, [P, P * len(sums), PACK], BF16)
            for j, acc in enumerate(sums):
                hid_t = sbuf("hid_t%d" % (r0 + P * j), [P, 2, P, 2], BF16)
                nc.vector.tensor_tensor(
                    hid_t[:], acc[:].rearrange("r (p u e) -> r u p e", u=2, e=2), unit_neg[:], MULT
                )
                words = hid_t[:].rearrange("r u p e -> r (u p e)").bitcast(F32)
                back = bank(back_banks[(r0 // P + j) % len(back_banks)])
                for u in range(2):
                    nc.tensor.transpose(back[:, P * u : P * (u + 1)], words[:, P * u : P * (u + 1)], ident[:])
                nc.scalar.copy(
                    hid[:, P * j : P * (j + 1), :].bitcast(F32),
                    back[:, 0 : 2 * P].rearrange("p (u r) -> p r u", u=2),
                )
            return hid

        def quantised(hid, r0):
            width = hid.shape[1]
            codes = sbuf("hid_codes%d" % r0, [P, width], U32)
            scales = sbuf("hid_scales%d" % r0, [P, width], U8)
            nc.vector.quantize_mx(
                out=codes[:].bitcast(FP8X4), scales=scales[:], in_=hid[:].rearrange("p r t -> p (r t)")
            )
            return codes, scales

        out_rows = out_0.rearrange("(p t) r -> p t r", t=PACK)
        out_words = out_1[0].rearrange("p r b -> p (r b)").bitcast(I32)
        out_codes = sbuf("out_codes", [P, U], I32)
        out_scales = sbuf("out_scales", [P, U], U8)

        def result(codes, scales, r0, out_banks, scalar_rounds):
            width = codes.shape[1]
            out_f = sbuf("out_f%d" % r0, [P, PACK, width], F32)
            out_b = sbuf("out_b%d" % r0, [P, width, PACK], BF16)
            for j in range(width // P):
                cols = slice(P * j, P * (j + 1))
                acc = bank(out_banks[j])
                for t in range(PACK):
                    nc.tensor.matmul_mx(
                        out=acc[:, P * t : P * (t + 1)],
                        lhsT=dealt_w[:, t, :, :].rearrange("k j b -> k (j b)").bitcast(FP4X4),
                        lhsT_scale=dealt_s[:, t, :],
                        rhs=codes[:, cols].bitcast(FP8X4),
                        rhs_scale=scales[:, cols],
                        start=True,
                        stop=True,
                    )
                nc.scalar.copy(out_f[:, :, cols], acc[:].rearrange("p (t r) -> p t r", t=PACK))
                if scalar_rounds:
                    nc.scalar.copy(out_b[:, cols, :], acc[:].rearrange("p (t r) -> p r t", t=PACK))
            nc.sync.dma_start(out=out_rows[:, :, r0 : r0 + width], in_=out_f[:])
            if not scalar_rounds:
                nc.vector.tensor_copy(out_b[:], out_f[:].rearrange("p t r -> p r t"))
            return out_b

        def planes(out_b, r0):
            width = out_b.shape[1]
            nc.vector.quantize_mx(
                out=out_codes[:, r0 : r0 + width].bitcast(FP8X4),
                scales=out_scales[:, r0 : r0 + width],
                in_=out_b[:].rearrange("p r t -> p (r t)"),
            )

        def store_codes(r0, r1):
            nc.sync.dma_start(out=out_words[:, r0:r1], in_=out_codes[:, r0:r1])

        sums = [bank(b) for b in SUM_BANKS]
        y_products()
        for t in range(TILES):
            z_product(t)
            if t == 0:
                deal_w3()
            look_up(0, t, 0)
            look_up(0, t, 1)
            add_up(sums, 0, t)

        look_up(1, 0, 0)
        look_up(1, 0, 1)
        halves = [quantised(rounded(sums[2 * h : 2 * h + 2], HALF * h, (0, 1)), HALF * h) for h in range(2)]
        sums = [bank(b) for b in SUM_BANKS]
        add_up(sums, 1, 0)
        look_up(1, 1, 0, buffer="hid_t0")
        look_up(1, 1, 1, buffer="hid_t%d" % P)
        add_up(sums, 1, 1)
        look_up(1, 2, 0, buffer="hid_t%d" % (2 * P))
        look_up(1, 2, 1, buffer="hid_t%d" % (3 * P))
        first_out = [result(*halves[0], 0, (2, 3), True)]
        add_up(sums, 1, 2)
        look_up(1, 3, 0)
        look_up(1, 3, 1, pieces=2)
        first_out.append(result(*halves[1], HALF, (2, 3), True))
        add_up(sums, 1, 3)

        starts = [CHUNK + P * j for j in range(BLOCKS)]
        hids = [rounded(sums[j : j + 1], starts[j], (0, 1, 2, 3)) for j in range(BLOCKS)]
        blocks = [quantised(hids[j], starts[j]) for j in range(BLOCKS)]
        for h in range(2):
            planes(first_out[h], HALF * h)
        store_codes(0, CHUNK)
        for j in range(BLOCKS):
            last = j == BLOCKS - 1
            planes(result(*blocks[j], starts[j], SUM_BANKS[j : j + 1], last), starts[j])
            if j == BLOCKS - 2:
                store_codes(CHUNK, starts[-1])
        store_codes(starts[-1], U)

        for q in range(4):
            queue = nc.sync if q % 2 else nc.scalar
            queue.dma_start(
                out=out_2[0, 4 * q : 4 * q + 4, :].bitcast(I32),
                in_=out_scales[32 * q : 32 * q + 4, :].bitcast(I32),
            )
